import numpy as np
import ml_dtypes


def mxq(x, axis, fmt="e4m3"):
    dtype, down = {"e4m3": (ml_dtypes.float8_e4m3fn, 7), "e5m2": (ml_dtypes.float8_e5m2, 14)}[fmt]
    v = np.moveaxis(np.asarray(x, np.float32).astype(ml_dtypes.bfloat16).astype(np.float64), axis, -1)
    blocks = v.reshape(v.shape[:-1] + (-1, 32))
    amax = np.abs(blocks).max(-1, keepdims=True)
    byte = np.maximum(np.where(amax > 0, np.frexp(amax)[1] - 1 + 127, 0) - down, 1)
    scale = np.exp2(byte - 127.0)
    codes = (blocks / scale).astype(np.float32).astype(dtype).astype(np.float64)
    return np.moveaxis((codes * scale).reshape(v.shape), -1, axis)


WIDE = False


def mx_kscale(k):
    if not WIDE:
        return np.ones(k)
    levels = np.array([10, -10, 5, -5, 0])
    if k % 512:
        return np.exp2(np.random.permutation(np.resize(levels, k // 32))).repeat(32)
    a = np.empty((k // 512, 16))
    for p in range(k // 512):
        a[p, :8] = np.random.permutation(np.resize(levels, 8))
        for g in range(8):
            far = levels[np.abs(levels - a[p, g]) >= 10]
            a[p, g + 8] = far[np.random.randint(len(far))]
    return np.exp2(a.ravel()).repeat(32)


def f64(x):
    return np.asarray(x).astype(np.float64)


def striped8(idx):
    return np.asarray(idx).reshape(8, -1, 16).transpose(0, 2, 1).reshape(128, -1).astype(np.uint16)


def unstriped8(offs):
    return offs.reshape(8, 16, -1).transpose(0, 2, 1).reshape(8, -1).astype(np.int64)


def pick8(x, idx, run):
    r = np.arange(len(x))
    return x[r[:, None], idx[r % (8 * run) // run]]


E2M1 = np.array([0.0, 0.5, 1.0, 1.5, 2.0, 3.0, 4.0, 6.0, -0.0, -0.5, -1.0, -1.5, -2.0, -3.0, -4.0, -6.0])


def pack_weight(w, fmt):
    k, n = w.shape
    w = f64(np.asarray(w, np.float32).astype(ml_dtypes.bfloat16)).reshape(k // 32, 32, n)
    amax = np.abs(w).max(1)
    if fmt == "e4m3":
        byte = np.frexp(amax)[1] - 1 + 127 - 7
    else:
        mant, ex = np.frexp(amax / 6.0)
        byte = np.where(mant > 0.5, ex, ex - 1) + 127
    byte = np.clip(np.where(amax > 0, byte, 1), 1, 254)
    scaled = (w * np.exp2(127.0 - byte)[:, None, :]).reshape(k, n).astype(np.float32)
    by_word = np.ascontiguousarray(scaled.reshape(k // 512, 128, 4, n).transpose(0, 1, 3, 2))
    if fmt == "e4m3":
        words = by_word.astype(ml_dtypes.float8_e4m3fn).view(np.uint8)
    else:
        c = by_word.astype(ml_dtypes.float4_e2m1fn).view(np.uint8) & 0xF
        words = (c[..., 0::2] | (c[..., 1::2] << 4)).reshape(k // 512, 128, 2 * n)
    return np.ascontiguousarray(words), np.ascontiguousarray(byte.astype(np.uint8).reshape(k // 512, 16, n))


def unpack_weight(words, scales, fmt):
    g, _, n = scales.shape
    words = np.ascontiguousarray(words).reshape(g, 128, n, -1)
    if fmt == "e4m3":
        vals = words.view(ml_dtypes.float8_e4m3fn).astype(np.float64)
    else:
        nib = np.empty((g, 128, n, 4), np.uint8)
        nib[..., 0::2] = words & 0xF
        nib[..., 1::2] = words >> 4
        vals = E2M1[nib]
    vals = vals * np.repeat(np.exp2(scales.astype(np.float64) - 127.0), 8, axis=1)[..., None]
    return vals.transpose(0, 1, 3, 2).reshape(g * 512, n)


def sigmoid(v):
    return 1.0 / (1.0 + np.exp(-v))


D, V, Q, I = 512, 2048, 128, 512


def setup_inputs():
    n = np.random.standard_normal
    idx = np.stack([np.random.permutation(V)[:I] for _ in range(8)])
    idx2 = np.stack([np.random.permutation(V)[:I] for _ in range(8)])
    fd = mx_kscale(D)
    vocp = pack_weight(n((D, V)) / fd[:, None], "e4m3")
    return {
        "hid": (n((D, Q)) * 1.0 / np.sqrt(D) * fd[:, None]).astype(np.float32),
        "voc_words": vocp[0],
        "voc_scales": vocp[1],
        "margin": (np.random.uniform(0.0, 1.0, (1, I))).astype(np.float32),
        "steep": (np.random.uniform(1.0, 3.0, (Q, 1))).astype(np.float32),
        "old": (0.5 * n((Q, V))).astype(np.float32),
        "offs": striped8(idx),
        "offs2": striped8(idx2),
    }


def reference(hid, voc_words, voc_scales, margin, steep, old, offs, offs2):
    idx = unstriped8(offs)
    idx2 = unstriped8(offs2)
    vocu = unpack_weight(voc_words, voc_scales, "e4m3")
    hidq = mxq(f64(hid), 0, "e4m3")
    a = hidq.T @ vocu
    b = pick8(a, idx2, 16) - pick8(a, idx, 16)
    db = sigmoid((b + f64(margin)) * f64(steep)) * f64(steep)
    s1 = np.zeros((Q, V))
    s1[np.arange(Q)[:, None], idx2[np.arange(Q) % 128 // 16]] = db
    e2 = db * (-1.0)
    s2 = np.zeros((Q, V))
    s2[np.arange(Q)[:, None], idx[np.arange(Q) % 128 // 16]] = e2
    da = s1 + s2
    y = da + f64(old)
    return y

@@ -1,0 +1,187 @@
+from contextlib import ExitStack
+
+import concourse.mybir as mybir
+from concourse.masks import make_identity
+
+F32 = mybir.dt.float32
+BF16 = mybir.dt.bfloat16
+I32 = mybir.dt.int32
+U32 = mybir.dt.uint32
+U16 = mybir.dt.uint16
+U8 = mybir.dt.uint8
+FP8X4 = mybir.dt.float8_e4m3fn_x4
+ALU = mybir.AluOpType
+ACT = mybir.ActivationFunctionType
+
+P = 128
+PACK = 4
+D, V, Q, SLOTS = 512, 2048, 128, 512
+BANK = 512
+LIST_COLS = SLOTS // 16
+FLOPS = 2 * D * Q * V
+
+WORD_LOAD = 512
+SCORE_PIECES = (512, 512, 256, 256, 256, 128, 128)
+FIRST_SLOTS = 128
+TURNED_BANKS = 3
+OUT_PIECES = ((0, 256), (256, 256), (512, 512), (1536, 512), (1024, 256), (1280, 256))
+
+
+def tile_attend_bpairmargin_heads_kernel(tc, hid, voc_words, voc_scales, margin, steep, old, offs, offs2, out):
+    nc = tc.nc
+    with ExitStack() as ctx:
+        keep = ctx.enter_context(tc.tile_pool(name="keep", bufs=1))
+        psum = ctx.enter_context(tc.psum_pool(name="psum", bufs=1))
+
+        def bank(number, name):
+            return psum.tile([P, BANK], F32, name=name, tag="bank%d" % number)
+
+        voc_planes = keep.tile([P, BANK], U8, align_bytes=64)
+        nc.vector.memset(voc_planes[:].bitcast(I32), 0)
+        s1 = keep.tile([P, V], F32)
+        nc.vector.memset(s1[:], 0.0)
+        ident = keep.tile([P, P], F32)
+        make_identity(nc, ident[:])
+
+        margin_cols = keep.tile([P, PACK], F32, align_bytes=64, tag="margin_then_codes")
+        nc.sync.dma_start(out=margin_cols[:], in_=margin[0].rearrange("(p t) -> p t", t=PACK))
+        hid_rows = keep.tile([P, PACK, Q], F32)
+        nc.sync.dma_start(out=hid_rows[:], in_=hid.rearrange("(p t) q -> p t q", t=PACK))
+        scale_rows = voc_scales[0].bitcast(I32)
+        for quad in range(4):
+            nc.sync.dma_start(
+                out=voc_planes[32 * quad : 32 * quad + 16, :].bitcast(I32),
+                in_=scale_rows[4 * quad : 4 * quad + 4, :].rearrange("r (j c) -> j r c", j=4),
+            )
+        word_rows = voc_words[0].rearrange("p n t -> p (n t)").bitcast(I32)
+        voc_codes = []
+        for c0 in range(0, V, WORD_LOAD):
+            codes = keep.tile([P, WORD_LOAD], I32, name="voc_codes_%d" % c0, tag="words_%d" % c0, align_bytes=64)
+            nc.sync.dma_start(out=codes[:], in_=word_rows[:, c0 : c0 + WORD_LOAD])
+            voc_codes.append(codes)
+        steep_col = keep.tile([P, 1], F32)
+        nc.sync.dma_start(out=steep_col[:], in_=steep)
+        first_list = keep.tile([P, LIST_COLS], U16)
+        nc.sync.dma_start(first_list[:], offs)
+        second_list = keep.tile([P, LIST_COLS], U16)
+        nc.sync.dma_start(second_list[:], offs2)
+        old_rows = keep.tile([P, V], F32)
+        nc.sync.dma_start(out=old_rows[:], in_=old)
+
+        margin_bank = bank(1, "margin_bank")
+        for t in range(PACK):
+            nc.tensor.transpose(
+                margin_bank[:, t * P : (t + 1) * P], margin_cols[:, t : t + 1].to_broadcast([P, P]), ident[:]
+            )
+        margin_rows = keep.tile([P, SLOTS], F32)
+        nc.scalar.copy(
+            margin_rows[:].rearrange("p (n t) -> p n t", t=PACK),
+            margin_bank[:].rearrange("p (t n) -> p n t", t=PACK),
+        )
+
+        hid_grouped = keep.tile([P, Q * PACK], BF16, align_bytes=64, tag="grouped_then_s2")
+        nc.vector.tensor_copy(
+            out=hid_grouped[:].rearrange("p (c i t) -> p c t i", i=4, t=PACK),
+            in_=hid_rows[:].rearrange("p t (c i) -> p c t i", i=4),
+        )
+        hid_codes = keep.tile([P, Q], U32, align_bytes=64, tag="margin_then_codes")
+        hid_plane = keep.tile([P, Q], U8, align_bytes=64)
+        nc.vector.quantize_mx(out=hid_codes[:].bitcast(FP8X4), scales=hid_plane[:], in_=hid_grouped[:])
+
+        s2 = keep.tile([P, V], F32, align_bytes=64, tag="grouped_then_s2")
+        nc.gpsimd.memset(s2[:], 0.0)
+
+        scores = keep.tile([P, V], F32)
+        c0 = 0
+        for piece, width in enumerate(SCORE_PIECES):
+            score_bank = bank(piece, "score_bank_%d" % piece)
+            plane, in_plane = divmod(c0, BANK)
+            load, in_load = divmod(c0, WORD_LOAD)
+            nc.tensor.matmul_mx(
+                out=score_bank[:, :width],
+                lhsT=hid_codes[:].bitcast(FP8X4),
+                lhsT_scale=hid_plane[:],
+                rhs=voc_codes[load][:, in_load : in_load + width].bitcast(FP8X4),
+                rhs_scale=voc_planes[4 * plane :, in_plane : in_plane + width],
+                start=True,
+                stop=True,
+            )
+            if piece % 2 == 0:
+                nc.vector.tensor_copy(scores[:, c0 : c0 + width], score_bank[:, :width])
+            else:
+                nc.scalar.copy(scores[:, c0 : c0 + width], score_bank[:, :width])
+            c0 = c0 + width
+
+        steep_rows = keep.tile([P, SLOTS - FIRST_SLOTS], F32, tag="words_%d" % (V - WORD_LOAD), align_bytes=64)
+        nc.scalar.copy(steep_rows[:], steep_col[:].to_broadcast([P, SLOTS - FIRST_SLOTS]))
+
+        minus_steep_rows = keep.tile([P, FIRST_SLOTS], F32)
+        nc.scalar.mul(minus_steep_rows[:], steep_rows[:, :FIRST_SLOTS], -1.0)
+
+        turned_banks = []
+        for b in range(TURNED_BANKS):
+            turned = bank(4 + b, "turned_bank_%d" % b)
+            for j in range(BANK // P):
+                nc.tensor.matmul(
+                    turned[:, j * P : (j + 1) * P],
+                    lhsT=old_rows[:, b * BANK + j * P : b * BANK + (j + 1) * P],
+                    rhs=ident[:],
+                    is_transpose=True,
+                    start=(j == 0),
+                    stop=False,
+                )
+            turned_banks.append(turned)
+
+        lowered = keep.tile([P, SLOTS], F32)
+        nc.vector.tensor_tensor(lowered[:], scores[:].indirect(first_list[:]), margin_rows[:], ALU.subtract)
+        gap = keep.tile([P, SLOTS], F32)
+        nc.vector.tensor_tensor(gap[:], scores[:].indirect(second_list[:]), lowered[:], ALU.subtract)
+
+        sig = keep.tile([P, SLOTS], F32)
+        head, tail = slice(0, FIRST_SLOTS), slice(FIRST_SLOTS, SLOTS)
+        head_cols, tail_cols = slice(0, FIRST_SLOTS // 16), slice(FIRST_SLOTS // 16, LIST_COLS)
+        nc.scalar.activation(sig[:, head], gap[:, head], ACT.Sigmoid, scale=steep_col[:])
+        nc.vector.tensor_tensor(
+            s1[:].indirect(second_list[:, head_cols]), sig[:, head], steep_rows[:, :FIRST_SLOTS], ALU.mult
+        )
+        nc.vector.tensor_tensor(s2[:].indirect(first_list[:, head_cols]), sig[:, head], minus_steep_rows[:], ALU.mult)
+        nc.scalar.activation(sig[:, tail], gap[:, tail], ACT.Sigmoid, scale=steep_col[:])
+        nc.vector.tensor_tensor(s1[:].indirect(second_list[:, tail_cols]), sig[:, tail], steep_rows[:], ALU.mult)
+        e2_tail = keep.tile([P, SLOTS - FIRST_SLOTS], F32)
+        nc.scalar.activation(e2_tail[:], sig[:, tail], ACT.Copy, scale=minus_steep_rows[:, 0:1])
+        nc.vector.tensor_copy(s2[:].indirect(first_list[:, tail_cols]), e2_tail[:])
+
+        turned_sums = []
+        for b in range(TURNED_BANKS):
+            turned = turned_banks[b]
+            for j in range(BANK // P):
+                nc.tensor.matmul(
+                    turned[:, j * P : (j + 1) * P],
+                    lhsT=s1[:, b * BANK + j * P : b * BANK + (j + 1) * P],
+                    rhs=ident[:],
+                    is_transpose=True,
+                    start=False,
+                    stop=(j == BANK // P - 1),
+                )
+            turned_sum = keep.tile([P, BANK], F32, name="turned_sum_%d" % b)
+            nc.scalar.copy(turned_sum[:], turned[:])
+            turned_sums.append(turned_sum)
+        partial_banks = []
+        for b in range(TURNED_BANKS):
+            turned_sum = turned_sums[b]
+            partial = bank((7 + b) % 8, "partial_bank_%d" % b)
+            for j in range(BANK // P):
+                nc.tensor.transpose(partial[:, j * P : (j + 1) * P], turned_sum[:, j * P : (j + 1) * P], ident[:])
+            partial_banks.append(partial)
+
+        rest = keep.tile([P, V - TURNED_BANKS * BANK], F32)
+        nc.gpsimd.tensor_tensor(rest[:], s1[:, TURNED_BANKS * BANK :], old_rows[:, TURNED_BANKS * BANK :], ALU.add)
+        partial_banks.append(rest)
+
+        for piece, (c0, width) in enumerate(OUT_PIECES):
+            b, in_bank = divmod(c0, BANK)
+            result = keep.tile([P, width], F32, name="result_%d" % piece)
+            nc.vector.tensor_tensor(
+                result[:], partial_banks[b][:, in_bank : in_bank + width], s2[:, c0 : c0 + width], ALU.add
+            )
+            nc.sync.dma_start(out=out[:, c0 : c0 + width], in_=result[:])

@@ -56,7 +56,7 @@ def tile_attend_bpairmargin_heads_kernel(tc, hid, voc_words, voc_scales, margin,
         word_rows = voc_words[0].rearrange("p n t -> p (n t)").bitcast(I32)
         voc_codes = []
         for c0 in range(0, V, WORD_LOAD):
-            codes = keep.tile([P, WORD_LOAD], I32, name="voc_codes_%d" % c0, tag="words_%d" % c0, align_bytes=64)
+            codes = keep.tile([P, WORD_LOAD], I32, name="voc_codes_%d" % c0, align_bytes=64)
             nc.sync.dma_start(out=codes[:], in_=word_rows[:, c0 : c0 + WORD_LOAD])
             voc_codes.append(codes)
         steep_col = keep.tile([P, 1], F32)
@@ -68,12 +68,12 @@ def tile_attend_bpairmargin_heads_kernel(tc, hid, voc_words, voc_scales, margin,
         old_rows = keep.tile([P, V], F32)
         nc.sync.dma_start(out=old_rows[:], in_=old)
 
-        margin_bank = bank(1, "margin_bank")
+        margin_bank = bank(5, "margin_bank")
         for t in range(PACK):
             nc.tensor.transpose(
                 margin_bank[:, t * P : (t + 1) * P], margin_cols[:, t : t + 1].to_broadcast([P, P]), ident[:]
             )
-        margin_rows = keep.tile([P, SLOTS], F32)
+        margin_rows = keep.tile([P, SLOTS], F32, tag="margin_then_minus_steep")
         nc.scalar.copy(
             margin_rows[:].rearrange("p (n t) -> p n t", t=PACK),
             margin_bank[:].rearrange("p (t n) -> p n t", t=PACK),
@@ -112,12 +112,6 @@ def tile_attend_bpairmargin_heads_kernel(tc, hid, voc_words, voc_scales, margin,
                 nc.scalar.copy(scores[:, c0 : c0 + width], score_bank[:, :width])
             c0 = c0 + width
 
-        steep_rows = keep.tile([P, SLOTS - FIRST_SLOTS], F32, tag="words_%d" % (V - WORD_LOAD), align_bytes=64)
-        nc.scalar.copy(steep_rows[:], steep_col[:].to_broadcast([P, SLOTS - FIRST_SLOTS]))
-
-        minus_steep_rows = keep.tile([P, FIRST_SLOTS], F32)
-        nc.scalar.mul(minus_steep_rows[:], steep_rows[:, :FIRST_SLOTS], -1.0)
-
         turned_banks = []
         for b in range(TURNED_BANKS):
             turned = bank(4 + b, "turned_bank_%d" % b)
@@ -132,10 +126,15 @@ def tile_attend_bpairmargin_heads_kernel(tc, hid, voc_words, voc_scales, margin,
                 )
             turned_banks.append(turned)
 
-        lowered = keep.tile([P, SLOTS], F32)
+        lowered = keep.tile([P, SLOTS], F32, tag="lowered_then_steep")
         nc.vector.tensor_tensor(lowered[:], scores[:].indirect(first_list[:]), margin_rows[:], ALU.subtract)
+        minus_steep_rows = keep.tile([P, FIRST_SLOTS], F32, tag="margin_then_minus_steep")
+        nc.vector.tensor_scalar_mul(minus_steep_rows[:], steep_col[:].to_broadcast([P, FIRST_SLOTS]), -1.0)
         gap = keep.tile([P, SLOTS], F32)
         nc.vector.tensor_tensor(gap[:], scores[:].indirect(second_list[:]), lowered[:], ALU.subtract)
+
+        steep_rows = keep.tile([P, SLOTS - FIRST_SLOTS], F32, tag="lowered_then_steep")
+        nc.vector.tensor_copy(steep_rows[:], steep_col[:].to_broadcast([P, SLOTS - FIRST_SLOTS]))
 
         sig = keep.tile([P, SLOTS], F32)
         head, tail = slice(0, FIRST_SLOTS), slice(FIRST_SLOTS, SLOTS)

@@ -13,18 +13,23 @@ FP8X4 = mybir.dt.float8_e4m3fn_x4
 ALU = mybir.AluOpType
 ACT = mybir.ActivationFunctionType
 
-P = 128
-PACK = 4
 D, V, Q, SLOTS = 512, 2048, 128, 512
-BANK = 512
-LIST_COLS = SLOTS // 16
 FLOPS = 2 * D * Q * V
 
-WORD_LOAD = 512
+P = 128
+PACK = 4
+BANK = 512
+QUADRANT = 32
+SCALE_ROWS = 4
+PER_LIST_COLUMN = 16
+STRETCHES = V // BANK
+
 SCORE_PIECES = (512, 512, 256, 256, 256, 128, 128)
-FIRST_SLOTS = 128
+HEAD_SLOTS = 128
 TURNED_BANKS = 3
-OUT_PIECES = ((0, 256), (256, 256), (512, 512), (1536, 512), (1024, 256), (1280, 256))
+TURNED_COLUMNS = TURNED_BANKS * BANK
+TURNED_BACK = ((0, 128), (128, 384), (512, 512), (1024, 256), (1280, 256))
+OUT_PIECES = ((0, 128), (128, 384), (512, 512), (1024, 256), (1536, 512), (1280, 128), (1408, 128))
 
 
 def tile_attend_bpairmargin_heads_kernel(tc, hid, voc_words, voc_scales, margin, steep, old, offs, offs2, out):
@@ -48,22 +53,24 @@ def tile_attend_bpairmargin_heads_kernel(tc, hid, voc_words, voc_scales, margin,
         hid_rows = keep.tile([P, PACK, Q], F32)
         nc.sync.dma_start(out=hid_rows[:], in_=hid.rearrange("(p t) q -> p t q", t=PACK))
         scale_rows = voc_scales[0].bitcast(I32)
-        for quad in range(4):
+        for quad in range(P // QUADRANT):
             nc.sync.dma_start(
-                out=voc_planes[32 * quad : 32 * quad + 16, :].bitcast(I32),
-                in_=scale_rows[4 * quad : 4 * quad + 4, :].rearrange("r (j c) -> j r c", j=4),
+                out=voc_planes[QUADRANT * quad : QUADRANT * quad + STRETCHES * SCALE_ROWS, :].bitcast(I32),
+                in_=scale_rows[SCALE_ROWS * quad : SCALE_ROWS * (quad + 1), :].rearrange(
+                    "r (j c) -> j r c", j=STRETCHES
+                ),
             )
         word_rows = voc_words[0].rearrange("p n t -> p (n t)").bitcast(I32)
         voc_codes = []
-        for c0 in range(0, V, WORD_LOAD):
-            codes = keep.tile([P, WORD_LOAD], I32, name="voc_codes_%d" % c0, align_bytes=64)
-            nc.sync.dma_start(out=codes[:], in_=word_rows[:, c0 : c0 + WORD_LOAD])
+        for stretch in range(STRETCHES):
+            codes = keep.tile([P, BANK], I32, name="voc_codes_%d" % stretch, align_bytes=64)
+            nc.sync.dma_start(out=codes[:], in_=word_rows[:, stretch * BANK : (stretch + 1) * BANK])
             voc_codes.append(codes)
         steep_col = keep.tile([P, 1], F32)
         nc.sync.dma_start(out=steep_col[:], in_=steep)
-        first_list = keep.tile([P, LIST_COLS], U16)
+        first_list = keep.tile([P, SLOTS // PER_LIST_COLUMN], U16)
         nc.sync.dma_start(first_list[:], offs)
-        second_list = keep.tile([P, LIST_COLS], U16)
+        second_list = keep.tile([P, SLOTS // PER_LIST_COLUMN], U16)
         nc.sync.dma_start(second_list[:], offs2)
         old_rows = keep.tile([P, V], F32)
         nc.sync.dma_start(out=old_rows[:], in_=old)
@@ -73,7 +80,7 @@ def tile_attend_bpairmargin_heads_kernel(tc, hid, voc_words, voc_scales, margin,
             nc.tensor.transpose(
                 margin_bank[:, t * P : (t + 1) * P], margin_cols[:, t : t + 1].to_broadcast([P, P]), ident[:]
             )
-        margin_rows = keep.tile([P, SLOTS], F32, tag="margin_then_minus_steep")
+        margin_rows = keep.tile([P, SLOTS], F32)
         nc.scalar.copy(
             margin_rows[:].rearrange("p (n t) -> p n t", t=PACK),
             margin_bank[:].rearrange("p (t n) -> p n t", t=PACK),
@@ -92,25 +99,24 @@ def tile_attend_bpairmargin_heads_kernel(tc, hid, voc_words, voc_scales, margin,
         nc.gpsimd.memset(s2[:], 0.0)
 
         scores = keep.tile([P, V], F32)
-        c0 = 0
+        v0 = 0
         for piece, width in enumerate(SCORE_PIECES):
             score_bank = bank(piece, "score_bank_%d" % piece)
-            plane, in_plane = divmod(c0, BANK)
-            load, in_load = divmod(c0, WORD_LOAD)
+            stretch, in_stretch = divmod(v0, BANK)
             nc.tensor.matmul_mx(
                 out=score_bank[:, :width],
                 lhsT=hid_codes[:].bitcast(FP8X4),
                 lhsT_scale=hid_plane[:],
-                rhs=voc_codes[load][:, in_load : in_load + width].bitcast(FP8X4),
-                rhs_scale=voc_planes[4 * plane :, in_plane : in_plane + width],
+                rhs=voc_codes[stretch][:, in_stretch : in_stretch + width].bitcast(FP8X4),
+                rhs_scale=voc_planes[SCALE_ROWS * stretch :, in_stretch : in_stretch + width],
                 start=True,
                 stop=True,
             )
             if piece % 2 == 0:
-                nc.vector.tensor_copy(scores[:, c0 : c0 + width], score_bank[:, :width])
+                nc.vector.tensor_copy(scores[:, v0 : v0 + width], score_bank[:, :width])
             else:
-                nc.scalar.copy(scores[:, c0 : c0 + width], score_bank[:, :width])
-            c0 = c0 + width
+                nc.scalar.copy(scores[:, v0 : v0 + width], score_bank[:, :width])
+            v0 = v0 + width
 
         turned_banks = []
         for b in range(TURNED_BANKS):
@@ -128,34 +134,34 @@ def tile_attend_bpairmargin_heads_kernel(tc, hid, voc_words, voc_scales, margin,
 
         lowered = keep.tile([P, SLOTS], F32, tag="lowered_then_steep")
         nc.vector.tensor_tensor(lowered[:], scores[:].indirect(first_list[:]), margin_rows[:], ALU.subtract)
-        minus_steep_rows = keep.tile([P, FIRST_SLOTS], F32, tag="margin_then_minus_steep")
-        nc.vector.tensor_scalar_mul(minus_steep_rows[:], steep_col[:].to_broadcast([P, FIRST_SLOTS]), -1.0)
         gap = keep.tile([P, SLOTS], F32)
         nc.vector.tensor_tensor(gap[:], scores[:].indirect(second_list[:]), lowered[:], ALU.subtract)
 
-        steep_rows = keep.tile([P, SLOTS - FIRST_SLOTS], F32, tag="lowered_then_steep")
-        nc.vector.tensor_copy(steep_rows[:], steep_col[:].to_broadcast([P, SLOTS - FIRST_SLOTS]))
+        steep_rows = keep.tile([P, 2, HEAD_SLOTS], F32, tag="lowered_then_steep")
+        steep_spread = steep_col[:].to_broadcast([P, HEAD_SLOTS])
+        nc.vector.tensor_copy(steep_rows[:, 0, :], steep_spread)
+        nc.vector.tensor_scalar_mul(steep_rows[:, 1, :], steep_spread, -1.0)
 
         sig = keep.tile([P, SLOTS], F32)
-        head, tail = slice(0, FIRST_SLOTS), slice(FIRST_SLOTS, SLOTS)
-        head_cols, tail_cols = slice(0, FIRST_SLOTS // 16), slice(FIRST_SLOTS // 16, LIST_COLS)
+        head, tail = slice(0, HEAD_SLOTS), slice(HEAD_SLOTS, SLOTS)
+        head_cols = slice(0, HEAD_SLOTS // PER_LIST_COLUMN)
+        tail_cols = slice(HEAD_SLOTS // PER_LIST_COLUMN, SLOTS // PER_LIST_COLUMN)
         nc.scalar.activation(sig[:, head], gap[:, head], ACT.Sigmoid, scale=steep_col[:])
-        nc.vector.tensor_tensor(
-            s1[:].indirect(second_list[:, head_cols]), sig[:, head], steep_rows[:, :FIRST_SLOTS], ALU.mult
-        )
-        nc.vector.tensor_tensor(s2[:].indirect(first_list[:, head_cols]), sig[:, head], minus_steep_rows[:], ALU.mult)
+        nc.vector.tensor_tensor(s1[:].indirect(second_list[:, head_cols]), sig[:, head], steep_rows[:, 0, :], ALU.mult)
+        nc.vector.tensor_tensor(s2[:].indirect(first_list[:, head_cols]), sig[:, head], steep_rows[:, 1, :], ALU.mult)
         nc.scalar.activation(sig[:, tail], gap[:, tail], ACT.Sigmoid, scale=steep_col[:])
-        nc.vector.tensor_tensor(s1[:].indirect(second_list[:, tail_cols]), sig[:, tail], steep_rows[:], ALU.mult)
-        e2_tail = keep.tile([P, SLOTS - FIRST_SLOTS], F32)
-        nc.scalar.activation(e2_tail[:], sig[:, tail], ACT.Copy, scale=minus_steep_rows[:, 0:1])
+        db_tail = keep.tile([P, SLOTS - HEAD_SLOTS], F32)
+        nc.scalar.activation(db_tail[:], sig[:, tail], ACT.Copy, scale=steep_col[:])
+        nc.vector.tensor_copy(s1[:].indirect(second_list[:, tail_cols]), db_tail[:])
+        e2_tail = keep.tile([P, SLOTS - HEAD_SLOTS], F32)
+        nc.scalar.activation(e2_tail[:], db_tail[:], ACT.Copy, scale=-1.0)
         nc.vector.tensor_copy(s2[:].indirect(first_list[:, tail_cols]), e2_tail[:])
 
         turned_sums = []
         for b in range(TURNED_BANKS):
-            turned = turned_banks[b]
             for j in range(BANK // P):
                 nc.tensor.matmul(
-                    turned[:, j * P : (j + 1) * P],
+                    turned_banks[b][:, j * P : (j + 1) * P],
                     lhsT=s1[:, b * BANK + j * P : b * BANK + (j + 1) * P],
                     rhs=ident[:],
                     is_transpose=True,
@@ -163,24 +169,22 @@ def tile_attend_bpairmargin_heads_kernel(tc, hid, voc_words, voc_scales, margin,
                     stop=(j == BANK // P - 1),
                 )
             turned_sum = keep.tile([P, BANK], F32, name="turned_sum_%d" % b)
-            nc.scalar.copy(turned_sum[:], turned[:])
+            nc.scalar.copy(turned_sum[:], turned_banks[b][:])
             turned_sums.append(turned_sum)
-        partial_banks = []
-        for b in range(TURNED_BANKS):
-            turned_sum = turned_sums[b]
-            partial = bank((7 + b) % 8, "partial_bank_%d" % b)
-            for j in range(BANK // P):
-                nc.tensor.transpose(partial[:, j * P : (j + 1) * P], turned_sum[:, j * P : (j + 1) * P], ident[:])
-            partial_banks.append(partial)
 
-        rest = keep.tile([P, V - TURNED_BANKS * BANK], F32)
-        nc.gpsimd.tensor_tensor(rest[:], s1[:, TURNED_BANKS * BANK :], old_rows[:, TURNED_BANKS * BANK :], ALU.add)
-        partial_banks.append(rest)
+        partial_of = {}
+        for part, (v0, width) in enumerate(TURNED_BACK):
+            partial = bank((7 + part) % 8, "partial_bank_%d" % part)
+            for at in range(0, width, P):
+                b, in_bank = divmod(v0 + at, BANK)
+                nc.tensor.transpose(partial[:, at : at + P], turned_sums[b][:, in_bank : in_bank + P], ident[:])
+                partial_of[v0 + at] = (partial, at)
+        rest = keep.tile([P, V - TURNED_COLUMNS], F32)
+        nc.gpsimd.tensor_tensor(rest[:], s1[:, TURNED_COLUMNS:], old_rows[:, TURNED_COLUMNS:], ALU.add)
+        partial_of[TURNED_COLUMNS] = (rest, 0)
 
-        for piece, (c0, width) in enumerate(OUT_PIECES):
-            b, in_bank = divmod(c0, BANK)
+        for piece, (v0, width) in enumerate(OUT_PIECES):
+            partial, at = partial_of[v0]
             result = keep.tile([P, width], F32, name="result_%d" % piece)
-            nc.vector.tensor_tensor(
-                result[:], partial_banks[b][:, in_bank : in_bank + width], s2[:, c0 : c0 + width], ALU.add
-            )
-            nc.sync.dma_start(out=out[:, c0 : c0 + width], in_=result[:])
+            nc.vector.tensor_tensor(result[:], partial[:, at : at + width], s2[:, v0 : v0 + width], ALU.add)
+            nc.sync.dma_start(out=out[:, v0 : v0 + width], in_=result[:])

from contextlib import ExitStack

import concourse.mybir as mybir
from concourse.masks import make_identity

F32 = mybir.dt.float32
BF16 = mybir.dt.bfloat16
I32 = mybir.dt.int32
U32 = mybir.dt.uint32
U16 = mybir.dt.uint16
U8 = mybir.dt.uint8
FP8X4 = mybir.dt.float8_e4m3fn_x4
ALU = mybir.AluOpType
ACT = mybir.ActivationFunctionType

D, V, Q, SLOTS = 512, 2048, 128, 512
FLOPS = 2 * D * Q * V

P = 128
PACK = 4
BANK = 512
QUADRANT = 32
SCALE_ROWS = 4
PER_LIST_COLUMN = 16
STRETCHES = V // BANK

SCORE_PIECES = (512, 512, 256, 256, 256, 128, 128)
HEAD_SLOTS = 128
TURNED_BANKS = 3
TURNED_COLUMNS = TURNED_BANKS * BANK
TURNED_BACK = ((0, 128), (128, 384), (512, 512), (1024, 256), (1280, 256))
OUT_PIECES = ((0, 128), (128, 384), (512, 512), (1024, 256), (1536, 512), (1280, 128), (1408, 128))


def tile_attend_bpairmargin_heads_kernel(tc, hid, voc_words, voc_scales, margin, steep, old, offs, offs2, out):
    nc = tc.nc
    with ExitStack() as ctx:
        keep = ctx.enter_context(tc.tile_pool(name="keep", bufs=1))
        psum = ctx.enter_context(tc.psum_pool(name="psum", bufs=1))

        def bank(number, name):
            return psum.tile([P, BANK], F32, name=name, tag="bank%d" % number)

        voc_planes = keep.tile([P, BANK], U8, align_bytes=64)
        nc.vector.memset(voc_planes[:].bitcast(I32), 0)
        s1 = keep.tile([P, V], F32)
        nc.vector.memset(s1[:], 0.0)
        ident = keep.tile([P, P], F32)
        make_identity(nc, ident[:])

        margin_cols = keep.tile([P, PACK], F32, align_bytes=64, tag="margin_then_codes")
        nc.sync.dma_start(out=margin_cols[:], in_=margin[0].rearrange("(p t) -> p t", t=PACK))
        hid_rows = keep.tile([P, PACK, Q], F32)
        nc.sync.dma_start(out=hid_rows[:], in_=hid.rearrange("(p t) q -> p t q", t=PACK))
        scale_rows = voc_scales[0].bitcast(I32)
        for quad in range(P // QUADRANT):
            nc.sync.dma_start(
                out=voc_planes[QUADRANT * quad : QUADRANT * quad + STRETCHES * SCALE_ROWS, :].bitcast(I32),
                in_=scale_rows[SCALE_ROWS * quad : SCALE_ROWS * (quad + 1), :].rearrange(
                    "r (j c) -> j r c", j=STRETCHES
                ),
            )
        word_rows = voc_words[0].rearrange("p n t -> p (n t)").bitcast(I32)
        voc_codes = []
        for stretch in range(STRETCHES):
            codes = keep.tile([P, BANK], I32, name="voc_codes_%d" % stretch, align_bytes=64)
            nc.sync.dma_start(out=codes[:], in_=word_rows[:, stretch * BANK : (stretch + 1) * BANK])
            voc_codes.append(codes)
        steep_col = keep.tile([P, 1], F32)
        nc.sync.dma_start(out=steep_col[:], in_=steep)
        first_list = keep.tile([P, SLOTS // PER_LIST_COLUMN], U16)
        nc.sync.dma_start(first_list[:], offs)
        second_list = keep.tile([P, SLOTS // PER_LIST_COLUMN], U16)
        nc.sync.dma_start(second_list[:], offs2)
        old_rows = keep.tile([P, V], F32)
        nc.sync.dma_start(out=old_rows[:], in_=old)

        margin_bank = bank(5, "margin_bank")
        for t in range(PACK):
            nc.tensor.transpose(
                margin_bank[:, t * P : (t + 1) * P], margin_cols[:, t : t + 1].to_broadcast([P, P]), ident[:]
            )
        margin_rows = keep.tile([P, SLOTS], F32)
        nc.scalar.copy(
            margin_rows[:].rearrange("p (n t) -> p n t", t=PACK),
            margin_bank[:].rearrange("p (t n) -> p n t", t=PACK),
        )

        hid_grouped = keep.tile([P, Q * PACK], BF16, align_bytes=64, tag="grouped_then_s2")
        nc.vector.tensor_copy(
            out=hid_grouped[:].rearrange("p (c i t) -> p c t i", i=4, t=PACK),
            in_=hid_rows[:].rearrange("p t (c i) -> p c t i", i=4),
        )
        hid_codes = keep.tile([P, Q], U32, align_bytes=64, tag="margin_then_codes")
        hid_plane = keep.tile([P, Q], U8, align_bytes=64)
        nc.vector.quantize_mx(out=hid_codes[:].bitcast(FP8X4), scales=hid_plane[:], in_=hid_grouped[:])

        s2 = keep.tile([P, V], F32, align_bytes=64, tag="grouped_then_s2")
        nc.gpsimd.memset(s2[:], 0.0)

        scores = keep.tile([P, V], F32)
        v0 = 0
        for piece, width in enumerate(SCORE_PIECES):
            score_bank = bank(piece, "score_bank_%d" % piece)
            stretch, in_stretch = divmod(v0, BANK)
            nc.tensor.matmul_mx(
                out=score_bank[:, :width],
                lhsT=hid_codes[:].bitcast(FP8X4),
                lhsT_scale=hid_plane[:],
                rhs=voc_codes[stretch][:, in_stretch : in_stretch + width].bitcast(FP8X4),
                rhs_scale=voc_planes[SCALE_ROWS * stretch :, in_stretch : in_stretch + width],
                start=True,
                stop=True,
            )
            if piece % 2 == 0:
                nc.vector.tensor_copy(scores[:, v0 : v0 + width], score_bank[:, :width])
            else:
                nc.scalar.copy(scores[:, v0 : v0 + width], score_bank[:, :width])
            v0 = v0 + width

        turned_banks = []
        for b in range(TURNED_BANKS):
            turned = bank(4 + b, "turned_bank_%d" % b)
            for j in range(BANK // P):
                nc.tensor.matmul(
                    turned[:, j * P : (j + 1) * P],
                    lhsT=old_rows[:, b * BANK + j * P : b * BANK + (j + 1) * P],
                    rhs=ident[:],
                    is_transpose=True,
                    start=(j == 0),
                    stop=False,
                )
            turned_banks.append(turned)

        lowered = keep.tile([P, SLOTS], F32, tag="lowered_then_steep")
        nc.vector.tensor_tensor(lowered[:], scores[:].indirect(first_list[:]), margin_rows[:], ALU.subtract)
        gap = keep.tile([P, SLOTS], F32)
        nc.vector.tensor_tensor(gap[:], scores[:].indirect(second_list[:]), lowered[:], ALU.subtract)

        steep_rows = keep.tile([P, 2, HEAD_SLOTS], F32, tag="lowered_then_steep")
        steep_spread = steep_col[:].to_broadcast([P, HEAD_SLOTS])
        nc.vector.tensor_copy(steep_rows[:, 0, :], steep_spread)
        nc.vector.tensor_scalar_mul(steep_rows[:, 1, :], steep_spread, -1.0)

        sig = keep.tile([P, SLOTS], F32)
        head, tail = slice(0, HEAD_SLOTS), slice(HEAD_SLOTS, SLOTS)
        head_cols = slice(0, HEAD_SLOTS // PER_LIST_COLUMN)
        tail_cols = slice(HEAD_SLOTS // PER_LIST_COLUMN, SLOTS // PER_LIST_COLUMN)
        nc.scalar.activation(sig[:, head], gap[:, head], ACT.Sigmoid, scale=steep_col[:])
        nc.vector.tensor_tensor(s1[:].indirect(second_list[:, head_cols]), sig[:, head], steep_rows[:, 0, :], ALU.mult)
        nc.vector.tensor_tensor(s2[:].indirect(first_list[:, head_cols]), sig[:, head], steep_rows[:, 1, :], ALU.mult)
        nc.scalar.activation(sig[:, tail], gap[:, tail], ACT.Sigmoid, scale=steep_col[:])
        db_tail = keep.tile([P, SLOTS - HEAD_SLOTS], F32)
        nc.scalar.activation(db_tail[:], sig[:, tail], ACT.Copy, scale=steep_col[:])
        nc.vector.tensor_copy(s1[:].indirect(second_list[:, tail_cols]), db_tail[:])
        e2_tail = keep.tile([P, SLOTS - HEAD_SLOTS], F32)
        nc.scalar.activation(e2_tail[:], db_tail[:], ACT.Copy, scale=-1.0)
        nc.vector.tensor_copy(s2[:].indirect(first_list[:, tail_cols]), e2_tail[:])

        turned_sums = []
        for b in range(TURNED_BANKS):
            for j in range(BANK // P):
                nc.tensor.matmul(
                    turned_banks[b][:, j * P : (j + 1) * P],
                    lhsT=s1[:, b * BANK + j * P : b * BANK + (j + 1) * P],
                    rhs=ident[:],
                    is_transpose=True,
                    start=False,
                    stop=(j == BANK // P - 1),
                )
            turned_sum = keep.tile([P, BANK], F32, name="turned_sum_%d" % b)
            nc.scalar.copy(turned_sum[:], turned_banks[b][:])
            turned_sums.append(turned_sum)

        partial_of = {}
        for part, (v0, width) in enumerate(TURNED_BACK):
            partial = bank((7 + part) % 8, "partial_bank_%d" % part)
            for at in range(0, width, P):
                b, in_bank = divmod(v0 + at, BANK)
                nc.tensor.transpose(partial[:, at : at + P], turned_sums[b][:, in_bank : in_bank + P], ident[:])
                partial_of[v0 + at] = (partial, at)
        rest = keep.tile([P, V - TURNED_COLUMNS], F32)
        nc.gpsimd.tensor_tensor(rest[:], s1[:, TURNED_COLUMNS:], old_rows[:, TURNED_COLUMNS:], ALU.add)
        partial_of[TURNED_COLUMNS] = (rest, 0)

        for piece, (v0, width) in enumerate(OUT_PIECES):
            partial, at = partial_of[v0]
            result = keep.tile([P, width], F32, name="result_%d" % piece)
            nc.vector.tensor_tensor(result[:], partial[:, at : at + width], s2[:, v0 : v0 + width], ALU.add)
            nc.sync.dma_start(out=out[:, v0 : v0 + width], in_=result[:])
